import numpy as np
import ml_dtypes


def mxq(x, axis, fmt="e4m3"):
    dtype, down = {"e4m3": (ml_dtypes.float8_e4m3fn, 7), "e5m2": (ml_dtypes.float8_e5m2, 14)}[fmt]
    v = np.moveaxis(np.asarray(x, np.float32).astype(ml_dtypes.bfloat16).astype(np.float64), axis, -1)
    blocks = v.reshape(v.shape[:-1] + (-1, 32))
    amax = np.abs(blocks).max(-1, keepdims=True)
    byte = np.maximum(np.where(amax > 0, np.frexp(amax)[1] - 1 + 127, 0) - down, 1)
    scale = np.exp2(byte - 127.0)
    codes = (blocks / scale).astype(np.float32).astype(dtype).astype(np.float64)
    return np.moveaxis((codes * scale).reshape(v.shape), -1, axis)


WIDE = False


def mx_kscale(k):
    if not WIDE:
        return np.ones(k)
    levels = np.array([10, -10, 5, -5, 0])
    if k % 512:
        return np.exp2(np.random.permutation(np.resize(levels, k // 32))).repeat(32)
    a = np.empty((k // 512, 16))
    for p in range(k // 512):
        a[p, :8] = np.random.permutation(np.resize(levels, 8))
        for g in range(8):
            far = levels[np.abs(levels - a[p, g]) >= 10]
            a[p, g + 8] = far[np.random.randint(len(far))]
    return np.exp2(a.ravel()).repeat(32)


def f64(x):
    return np.asarray(x).astype(np.float64)


def striped(idx):
    return np.tile(idx.reshape(-1, 16).T, (8, 1)).astype(np.uint16)


def unstriped(offs):
    return offs[:16].T.reshape(-1).astype(np.int64)


def sigmoid(v):
    return 1.0 / (1.0 + np.exp(-np.maximum(v, -700.0)))


def d_sigmoid(v):
    s = 1.0 / (1.0 + np.exp(-np.maximum(v, -700.0)))
    return s * (1.0 - s)


K, T, E, C, H, N = 128, 640, 4, 128, 1024, 1536


def by_expert(wq, xq):
    return np.concatenate([wq[e].T @ xq[:, e * C:(e + 1) * C] for e in range(E)], axis=1)


def setup_inputs():
    n = np.random.standard_normal
    s = mx_kscale(N)[:, None]
    u = mx_kscale(H)
    return {
        "dyT": (n((N, T)) * s).astype(np.float32),
        "a1": n((H, E * C)).astype(np.float32),
        "a3": n((H, E * C)).astype(np.float32),
        "w2": (n((E, N, H)) / np.sqrt(N) / s[None] * u[None, None, :]).astype(np.float32),
        "w1": (n((E, H, K)) / np.sqrt(H) / u[None, :, None]).astype(np.float32),
        "w3": (n((E, H, K)) / np.sqrt(H) / u[None, :, None]).astype(np.float32),
        "gate": np.tile(np.random.uniform(0.2, 1.0, E * C), (N, 1)).astype(np.float32),
        "offs": striped(np.random.permutation(T)[:E * C]),
    }


def reference(dyT, a1, a3, w2, w1, w3, gate, offs):
    idx = unstriped(offs)
    gq = mxq(f64(gate) * f64(dyT)[:, idx], 0, "e4m3")
    dh = by_expert(mxq(f64(w2), 1, "e4m3"), gq)
    da1 = dh * f64(a3) * d_sigmoid(f64(a1))
    da3 = dh * sigmoid(f64(a1))
    dx = by_expert(mxq(f64(w1), 1, "e4m3"), mxq(da1, 0, "e4m3")) + by_expert(mxq(f64(w3), 1, "e4m3"), mxq(da3, 0, "e4m3"))
    out = np.zeros((K, T))
    out[:, idx] = dx
    return out

@@ -1,0 +1,352 @@
+from contextlib import ExitStack
+
+import concourse.mybir as mybir
+
+P = 128
+E, C, K, T, H, N = 4, 128, 128, 640, 1024, 1536
+S = E * C
+NP = N // 512
+HP = H // 512
+
+FLOPS = 2 * S * (N * H + 2 * H * K)
+BYTES = 4 * (N * T + 2 * H * S + E * N * H + 2 * E * H * K + S + K * T) + 2 * P * S // 16
+
+F32 = mybir.dt.float32
+BF16 = mybir.dt.bfloat16
+U32 = mybir.dt.uint32
+U16 = mybir.dt.uint16
+U8 = mybir.dt.uint8
+FP8X4 = mybir.dt.float8_e4m3fn_x4
+MULT = mybir.AluOpType.mult
+SIGMOID = mybir.ActivationFunctionType.Sigmoid
+
+
+def tile_moe_bdx_glu_sigmoid_kernel(tc, dyT, a1, a3, w2, w1, w3, gate, offs, out):
+    nc = tc.nc
+    with ExitStack() as ctx:
+        keep = ctx.enter_context(tc.tile_pool(name="keep", bufs=1))
+        ring = ctx.enter_context(tc.tile_pool(name="ring", bufs=6))
+        stage = ctx.enter_context(tc.tile_pool(name="stage", bufs=6))
+        dy_pool = ctx.enter_context(tc.tile_pool(name="dy", bufs=12))
+        codes_pool = ctx.enter_context(tc.tile_pool(name="codes", bufs=6))
+        work = ctx.enter_context(tc.tile_pool(name="work", bufs=2))
+        psum = ctx.enter_context(tc.psum_pool(name="psum", bufs=6))
+        psum_dx = ctx.enter_context(tc.psum_pool(name="psum_dx", bufs=2))
+
+        offsets = keep.tile([P, S // 16], U16, name="offsets")
+        nc.sync.dma_start(offsets[:], offs)
+        gate_t = keep.tile([P, S], F32, name="gate_t")
+        out_t = keep.tile([P, T], F32, name="out_t")
+        nc.gpsimd.memset(out_t[:], 0.0)
+        warm = keep.tile([P, 1], F32, name="warm")
+        nc.gpsimd.memset(warm[:], 0.0)
+        nc.scalar.activation(warm[:], warm[:], SIGMOID)
+
+        def load_dy(c):
+            view = dyT[512 * c : 512 * c + 512, :].rearrange("(p j) t -> p j t", j=4)
+            rows = []
+            for j in range(4):
+                row = dy_pool.tile([P, T], F32, tag="dy", align_bytes=64)
+                nc.sync.dma_start(row[:], view[:, j, :])
+                rows.append(row)
+            return rows
+
+        def load_w2(e, c, by_half=False):
+            raw = ring.tile([P, 4, H], F32, tag="raw")
+            view = w2[e, 512 * c : 512 * c + 512, :].rearrange("(p j) i -> p j i", j=4)
+            if by_half:
+                for h in range(HP):
+                    nc.sync.dma_start(raw[:, :, 512 * h : 512 * h + 512], view[:, :, 512 * h : 512 * h + 512])
+            else:
+                nc.sync.dma_start(raw[:], view)
+            return raw
+
+        def load_saved(a):
+            raw = ring.tile([P, HP, 4, S], F32, tag="raw")
+            nc.sync.dma_start(raw[:], a.rearrange("(h p j) s -> p h j s", h=HP, j=4))
+            return raw
+
+        g_codes = []
+        g_scales = []
+        for c in range(NP):
+            gc = keep.tile([P, S], U32, name=f"g_codes{c}", align_bytes=64)
+            gs = keep.tile([P, S], U8, name=f"g_scales{c}", align_bytes=64)
+            g_codes.append(gc)
+            g_scales.append(gs)
+
+        def gather(c, half):
+            cols = slice(256 * half, 256 * half + 256)
+            g4 = work.tile([P, 4, 256], F32)
+            for j in range(4):
+                nc.vector.tensor_tensor(
+                    g4[:, j, :], dy[c][j][:].indirect(offsets[:, 16 * half : 16 * half + 16]), gate_t[:, cols], MULT
+                )
+            return g4
+
+        def round_g(g4):
+            gb = stage.tile([P, 256, 4], BF16, tag="stage", align_bytes=64)
+            nc.vector.tensor_copy(
+                gb[:].rearrange("p (c i) j -> p c j i", i=4), g4[:].rearrange("p j (c i) -> p c j i", i=4)
+            )
+            return gb
+
+        def quantize_g(c, half, gb):
+            cols = slice(256 * half, 256 * half + 256)
+            nc.vector.quantize_mx(
+                out=g_codes[c][:, cols].bitcast(FP8X4), scales=g_scales[c][:, cols], in_=gb[:].rearrange("p s j -> p (s j)")
+            )
+
+        def copy_w2(raw, h, pieces):
+            st = stage.tile([P, 2048], BF16, tag="stage", align_bytes=64)
+            dst = st[:].rearrange("p (t m j) -> p m j t", t=4, j=4)
+            src = raw[:, :, 512 * h : 512 * h + 512].rearrange("p j (m t) -> p m j t", t=4)
+            for eng, lo, hi in pieces:
+                if eng == "v":
+                    nc.vector.tensor_copy(dst[:, lo:hi], src[:, lo:hi])
+                else:
+                    nc.scalar.copy(dst[:, lo:hi], src[:, lo:hi])
+            return st
+
+        def quantize_w2(st, codes, scales, h):
+            cols = slice(512 * h, 512 * h + 512)
+            nc.vector.quantize_mx(out=codes[:, cols].bitcast(FP8X4), scales=scales[:, cols], in_=st[:])
+
+        da_codes = {}
+        da_scales = {}
+
+        def hidden_mm(e, h):
+            wc, ws = w2_codes[e]
+            dh = psum.tile([P, 4, C], F32)
+            slots = slice(C * e, C * e + C)
+            for t in range(4):
+                cols = slice(512 * h + 128 * t, 512 * h + 128 * t + 128)
+                for c in range(NP):
+                    nc.tensor.matmul_mx(
+                        out=dh[:, t, :],
+                        lhsT=wc[c][:, cols].bitcast(FP8X4),
+                        lhsT_scale=ws[c][:, cols],
+                        rhs=g_codes[c][:, slots].bitcast(FP8X4),
+                        rhs_scale=g_scales[c][:, slots],
+                        start=(c == 0),
+                        stop=(c == NP - 1),
+                    )
+            return dh
+
+        def hidden_da(e, h, dh):
+            slots = slice(C * e, C * e + C)
+            da = work.tile([P, 2, C, 4], BF16, bufs=3, align_bytes=64)
+            for m, factor in ((1, s_t), (0, t_t)):
+                nc.vector.tensor_tensor(
+                    da[:, m].rearrange("p (c i) t -> p c t i", i=4),
+                    dh[:].rearrange("p t (c i) -> p c t i", i=4),
+                    factor[:, h, :, slots].rearrange("p t (c i) -> p c t i", i=4),
+                    MULT,
+                )
+            return da
+
+        def hidden_q(e, h, da):
+            dc = keep.tile([P, 2 * C], U32, name=f"da_codes{e}_{h}", align_bytes=64)
+            ds = keep.tile([P, 2 * C], U8, name=f"da_scales{e}_{h}", align_bytes=64)
+            nc.vector.quantize_mx(out=dc[:].bitcast(FP8X4), scales=ds[:], in_=da[:].rearrange("p m s t -> p (m s t)"))
+            da_codes[e, h] = dc
+            da_scales[e, h] = ds
+
+        def hidden(e):
+            dhs = [hidden_mm(e, h) for h in range(HP)]
+            das = [hidden_da(e, h, dhs[h]) for h in range(HP)]
+            for h in range(HP):
+                hidden_q(e, h, das[h])
+
+        def copy_w13(raw, st, el, m, h, eng):
+            src = raw[:, m, HP * el + h].rearrange("p j (c i) -> p c j i", i=4)
+            dst = st[:, m, h].rearrange("p (c i) j -> p c j i", i=4)
+            if eng == "v":
+                nc.vector.tensor_copy(dst, src)
+            else:
+                nc.scalar.copy(dst, src)
+
+        def codes_w13(e):
+            wc = dy_pool.tile([P, 2, HP, K], U32, tag="dy", align_bytes=64)
+            ws = keep.tile([P, 2, HP, K], U8, name=f"w13_scales{e}", align_bytes=64)
+            return wc, ws
+
+        def down(e, wc, ws, dxs, col):
+            dx = psum_dx.tile([P, C], F32)
+            order = [(m, h) for m in range(2) for h in range(HP)]
+            for n, (m, h) in enumerate(order):
+                nc.tensor.matmul_mx(
+                    out=dx[:],
+                    lhsT=wc[:, m, h, :].bitcast(FP8X4),
+                    lhsT_scale=ws[:, m, h, :],
+                    rhs=da_codes[e, h][:, C * m : C * m + C].bitcast(FP8X4),
+                    rhs_scale=da_scales[e, h][:, C * m : C * m + C],
+                    start=(n == 0),
+                    stop=(n == len(order) - 1),
+                )
+            nc.scalar.copy(dxs[:, col : col + C], dx[:])
+
+        def scatter(dxs, e0, ne):
+            nc.vector.tensor_copy(out_t[:].indirect(offsets[:, 8 * e0 : 8 * (e0 + ne)]), dxs[:])
+
+        w2_raw = {}
+        dy = []
+        nc.sync.dma_start(gate_t[:], gate[0:P, :])
+        for c in range(NP):
+            dy.append(load_dy(c))
+            w2_raw[0, c] = load_w2(0, c)
+        s_t = load_saved(a1)
+        t_t = load_saved(a3)
+        w2_raw[1, 0] = load_w2(1, 0)
+
+        raw13 = {}
+
+        def load_w13(e0, fine):
+            raw = ring.tile([P, 2, 2 * HP, 4, K], F32, tag="raw")
+            nc.sync.dma_start(raw[:, 0], w1[e0 : e0 + 2].rearrange("e (h p j) k -> p (e h) j k", h=HP, j=4))
+            if fine:
+                nc.sync.dma_start(raw[:, 1, 0:HP], w3[e0].rearrange("(h p j) k -> p h j k", h=HP, j=4))
+                for h in range(HP):
+                    nc.sync.dma_start(
+                        raw[:, 1, HP + h], w3[e0 + 1, 512 * h : 512 * h + 512, :].rearrange("(p j) k -> p j k", j=4)
+                    )
+            else:
+                nc.sync.dma_start(raw[:, 1], w3[e0 : e0 + 2].rearrange("e (h p j) k -> p (e h) j k", h=HP, j=4))
+            raw13[e0] = raw
+
+        def issue(load):
+            if load is None:
+                return
+            if load[0] == "w2":
+                w2_raw[load[1], load[2]] = load_w2(load[1], load[2], load[1:] == (3, 2))
+            else:
+                load_w13(load[1], load[1] == 2)
+
+        ALLS = [("s", 0, 128)]
+        ALLV = [("v", 0, 128)]
+        plan = {
+            0: [ALLS, ALLV, ALLS, ALLS, ALLS, ALLS],
+            1: [ALLS, ALLS, ALLS, ALLS, ALLS, ALLV],
+            2: [ALLS, ALLS, ALLS, ALLS, ALLS, ALLV],
+            3: [ALLS, ALLS, ALLS, ALLV, ALLS, [("s", 0, 44), ("v", 44, 128)]],
+        }
+        w2_codes = {e: ([], []) for e in range(E)}
+
+        def copies(e, c):
+            return [copy_w2(w2_raw[e, c], h, plan[e][2 * c + h]) for h in range(HP)]
+
+        def new_codes(e):
+            codes = codes_pool.tile([P, H], U32, align_bytes=64)
+            scales = codes_pool.tile([P, H], U8, align_bytes=64)
+            w2_codes[e][0].append(codes)
+            w2_codes[e][1].append(scales)
+
+        def quants(e, c, sts):
+            new_codes(e)
+            for h in range(HP):
+                quantize_w2(sts[h], w2_codes[e][0][c], w2_codes[e][1][c], h)
+
+        def copy_weights13(e, raw, el):
+            st = stage.tile([P, 2, HP, K, 4], BF16, tag="stage", align_bytes=64)
+            for m in range(2):
+                for h in range(HP):
+                    copy_w13(raw, st, el, m, h, "v" if m == 1 else "s")
+            return st
+
+        def quant_weights13(e, st, fine):
+            wc, ws = codes_w13(e)
+            if fine:
+                nc.vector.quantize_mx(
+                    out=wc[:, 0].rearrange("p h k -> p (h k)").bitcast(FP8X4),
+                    scales=ws[:, 0].rearrange("p h k -> p (h k)"),
+                    in_=st[:, 0].rearrange("p h k j -> p (h k j)"),
+                )
+                for h in range(HP):
+                    nc.vector.quantize_mx(
+                        out=wc[:, 1, h].bitcast(FP8X4), scales=ws[:, 1, h], in_=st[:, 1, h].rearrange("p k j -> p (k j)")
+                    )
+            else:
+                nc.vector.quantize_mx(
+                    out=wc[:].rearrange("p m h k -> p (m h k)").bitcast(FP8X4),
+                    scales=ws[:].rearrange("p m h k -> p (m h k)"),
+                    in_=st[:].rearrange("p m h k j -> p (m h k j)"),
+                )
+            return wc, ws
+
+        loads0 = [("w2", 1, 1), ("w2", 1, 2), ("w13", 0)]
+        gathers = [(c, half) for half in range(2) for c in range(NP)]
+        prev_g = None
+        prev_w = None
+        for n, (c, half) in enumerate(gathers):
+            g4 = gather(c, half)
+            if n < NP:
+                sts = copies(0, n)
+                issue(loads0[n])
+            gb = round_g(g4)
+            if prev_g is not None:
+                quantize_g(prev_g[0], prev_g[1], prev_g[2])
+            if prev_w is not None:
+                quants(0, prev_w[0], prev_w[1])
+            prev_g = (c, half, gb)
+            prev_w = (n, sts) if n < NP else None
+        for h in range(HP):
+            for j in range(4):
+                sneg = work.tile([P, S], F32)
+                nc.scalar.activation(sneg[:], s_t[:, h, j], SIGMOID, scale=-1.0)
+                nc.vector.tensor_tensor(t_t[:, h, j], sneg[:], t_t[:, h, j], MULT)
+                if h == 0 and j == 0:
+                    quantize_g(prev_g[0], prev_g[1], prev_g[2])
+            nc.scalar.activation(s_t[:, h], s_t[:, h], SIGMOID)
+        for h in range(HP):
+            nc.vector.tensor_tensor(t_t[:, h], s_t[:, h], t_t[:, h], MULT)
+
+        loads1 = [("w2", 2, 0), ("w2", 2, 1), ("w2", 2, 2)]
+        for c in range(NP):
+            now = copies(1, c)
+            issue(loads1[c])
+            if c == 0:
+                hidden(0)
+            else:
+                quants(1, c - 1, sts)
+            sts = now
+        st13 = [copy_weights13(0, raw13[0], 0), None]
+        quants(1, 2, sts)
+        st13[1] = copy_weights13(1, raw13[0], 1)
+        issue(("w2", 3, 0))
+        w13 = [quant_weights13(0, st13[0], False), None]
+        loads2 = [("w2", 3, 1), ("w2", 3, 2), ("w13", 2)]
+        dxs01 = keep.tile([P, 2 * C], F32, name="dxs01")
+        for c in range(NP):
+            now = copies(2, c)
+            issue(loads2[c])
+            if c == 0:
+                hidden(1)
+                w13[1] = quant_weights13(1, st13[1], False)
+                down(0, w13[0][0], w13[0][1], dxs01, 0)
+                down(1, w13[1][0], w13[1][1], dxs01, C)
+            else:
+                quants(2, c - 1, sts)
+            if c == 1:
+                scatter(dxs01, 0, 2)
+            sts = now
+        for c in range(NP):
+            now = copies(3, c)
+            if c == 0:
+                quants(2, 2, sts)
+            else:
+                quants(3, c - 1, sts)
+            if c == 1:
+                hidden(2)
+            sts = now
+        quants(3, 2, sts)
+        st2 = copy_weights13(2, raw13[2], 0)
+        hidden(3)
+        wc2, ws2 = quant_weights13(2, st2, False)
+        dxs2 = work.tile([P, C], F32, tag="dxs")
+        down(2, wc2, ws2, dxs2, 0)
+        st3 = copy_weights13(3, raw13[2], 1)
+        scatter(dxs2, 2, 1)
+        wc3, ws3 = quant_weights13(3, st3, True)
+        dxs3 = work.tile([P, C], F32, tag="dxs")
+        down(3, wc3, ws3, dxs3, 0)
+        scatter(dxs3, 3, 1)
+        nc.sync.dma_start(out, out_t[:])

@@ -42,311 +42,217 @@ def tile_moe_bdx_glu_sigmoid_kernel(tc, dyT, a1, a3, w2, w1, w3, gate, offs, out
         nc.gpsimd.memset(warm[:], 0.0)
         nc.scalar.activation(warm[:], warm[:], SIGMOID)
 
-        def load_dy(c):
-            view = dyT[512 * c : 512 * c + 512, :].rearrange("(p j) t -> p j t", j=4)
-            rows = []
-            for j in range(4):
-                row = dy_pool.tile([P, T], F32, tag="dy", align_bytes=64)
-                nc.sync.dma_start(row[:], view[:, j, :])
-                rows.append(row)
-            return rows
-
-        def load_w2(e, c, by_half=False):
-            raw = ring.tile([P, 4, H], F32, tag="raw")
-            view = w2[e, 512 * c : 512 * c + 512, :].rearrange("(p j) i -> p j i", j=4)
-            if by_half:
-                for h in range(HP):
-                    nc.sync.dma_start(raw[:, :, 512 * h : 512 * h + 512], view[:, :, 512 * h : 512 * h + 512])
-            else:
-                nc.sync.dma_start(raw[:], view)
-            return raw
-
-        def load_saved(a):
-            raw = ring.tile([P, HP, 4, S], F32, tag="raw")
-            nc.sync.dma_start(raw[:], a.rearrange("(h p j) s -> p h j s", h=HP, j=4))
-            return raw
-
-        g_codes = []
-        g_scales = []
-        for c in range(NP):
-            gc = keep.tile([P, S], U32, name=f"g_codes{c}", align_bytes=64)
-            gs = keep.tile([P, S], U8, name=f"g_scales{c}", align_bytes=64)
-            g_codes.append(gc)
-            g_scales.append(gs)
-
-        def gather(c, half):
-            cols = slice(256 * half, 256 * half + 256)
-            g4 = work.tile([P, 4, 256], F32)
-            for j in range(4):
-                nc.vector.tensor_tensor(
-                    g4[:, j, :], dy[c][j][:].indirect(offsets[:, 16 * half : 16 * half + 16]), gate_t[:, cols], MULT
-                )
-            return g4
-
-        def round_g(g4):
-            gb = stage.tile([P, 256, 4], BF16, tag="stage", align_bytes=64)
-            nc.vector.tensor_copy(
-                gb[:].rearrange("p (c i) j -> p c j i", i=4), g4[:].rearrange("p j (c i) -> p c j i", i=4)
-            )
-            return gb
-
-        def quantize_g(c, half, gb):
-            cols = slice(256 * half, 256 * half + 256)
-            nc.vector.quantize_mx(
-                out=g_codes[c][:, cols].bitcast(FP8X4), scales=g_scales[c][:, cols], in_=gb[:].rearrange("p s j -> p (s j)")
-            )
-
-        def copy_w2(raw, h, pieces):
-            st = stage.tile([P, 2048], BF16, tag="stage", align_bytes=64)
-            dst = st[:].rearrange("p (t m j) -> p m j t", t=4, j=4)
-            src = raw[:, :, 512 * h : 512 * h + 512].rearrange("p j (m t) -> p m j t", t=4)
-            for eng, lo, hi in pieces:
-                if eng == "v":
-                    nc.vector.tensor_copy(dst[:, lo:hi], src[:, lo:hi])
-                else:
-                    nc.scalar.copy(dst[:, lo:hi], src[:, lo:hi])
-            return st
-
-        def quantize_w2(st, codes, scales, h):
-            cols = slice(512 * h, 512 * h + 512)
-            nc.vector.quantize_mx(out=codes[:, cols].bitcast(FP8X4), scales=scales[:, cols], in_=st[:])
-
-        da_codes = {}
-        da_scales = {}
-
-        def hidden_mm(e, h):
-            wc, ws = w2_codes[e]
-            dh = psum.tile([P, 4, C], F32)
-            slots = slice(C * e, C * e + C)
-            for t in range(4):
-                cols = slice(512 * h + 128 * t, 512 * h + 128 * t + 128)
-                for c in range(NP):
-                    nc.tensor.matmul_mx(
-                        out=dh[:, t, :],
-                        lhsT=wc[c][:, cols].bitcast(FP8X4),
-                        lhsT_scale=ws[c][:, cols],
-                        rhs=g_codes[c][:, slots].bitcast(FP8X4),
-                        rhs_scale=g_scales[c][:, slots],
-                        start=(c == 0),
-                        stop=(c == NP - 1),
-                    )
-            return dh
-
-        def hidden_da(e, h, dh):
-            slots = slice(C * e, C * e + C)
-            da = work.tile([P, 2, C, 4], BF16, bufs=3, align_bytes=64)
-            for m, factor in ((1, s_t), (0, t_t)):
-                nc.vector.tensor_tensor(
-                    da[:, m].rearrange("p (c i) t -> p c t i", i=4),
-                    dh[:].rearrange("p t (c i) -> p c t i", i=4),
-                    factor[:, h, :, slots].rearrange("p t (c i) -> p c t i", i=4),
-                    MULT,
-                )
-            return da
-
-        def hidden_q(e, h, da):
-            dc = keep.tile([P, 2 * C], U32, name=f"da_codes{e}_{h}", align_bytes=64)
-            ds = keep.tile([P, 2 * C], U8, name=f"da_scales{e}_{h}", align_bytes=64)
-            nc.vector.quantize_mx(out=dc[:].bitcast(FP8X4), scales=ds[:], in_=da[:].rearrange("p m s t -> p (m s t)"))
-            da_codes[e, h] = dc
-            da_scales[e, h] = ds
-
-        def hidden(e):
-            dhs = [hidden_mm(e, h) for h in range(HP)]
-            das = [hidden_da(e, h, dhs[h]) for h in range(HP)]
-            for h in range(HP):
-                hidden_q(e, h, das[h])
-
-        def copy_w13(raw, st, el, m, h, eng):
-            src = raw[:, m, HP * el + h].rearrange("p j (c i) -> p c j i", i=4)
-            dst = st[:, m, h].rearrange("p (c i) j -> p c j i", i=4)
-            if eng == "v":
-                nc.vector.tensor_copy(dst, src)
-            else:
-                nc.scalar.copy(dst, src)
-
-        def codes_w13(e):
-            wc = dy_pool.tile([P, 2, HP, K], U32, tag="dy", align_bytes=64)
-            ws = keep.tile([P, 2, HP, K], U8, name=f"w13_scales{e}", align_bytes=64)
-            return wc, ws
-
-        def down(e, wc, ws, dxs, col):
-            dx = psum_dx.tile([P, C], F32)
-            order = [(m, h) for m in range(2) for h in range(HP)]
-            for n, (m, h) in enumerate(order):
-                nc.tensor.matmul_mx(
-                    out=dx[:],
-                    lhsT=wc[:, m, h, :].bitcast(FP8X4),
-                    lhsT_scale=ws[:, m, h, :],
-                    rhs=da_codes[e, h][:, C * m : C * m + C].bitcast(FP8X4),
-                    rhs_scale=da_scales[e, h][:, C * m : C * m + C],
-                    start=(n == 0),
-                    stop=(n == len(order) - 1),
-                )
-            nc.scalar.copy(dxs[:, col : col + C], dx[:])
-
-        def scatter(dxs, e0, ne):
-            nc.vector.tensor_copy(out_t[:].indirect(offsets[:, 8 * e0 : 8 * (e0 + ne)]), dxs[:])
-
-        w2_raw = {}
-        dy = []
+        ORDER = """l0 L0.0 l1 A0.0 A1.0 l2 L0.1 A0.1 A1.1 L0.2 L1.0
+G0.0 G0.1 R0.0 R0.1 C0.0.0 C0.0.1 L1.1 Q0.0 Q0.1 S0 G1.0 G1.1 T0 R1.0 R1.1 P0 W0.0.0 W0.0.1 Q1.0 Q1.1 G2.0 G2.1 C0.1.0 C0.1.1 L1.2 R2.0 R2.1 S1 T1 Q2.0 Q2.1 P1 W0.1.0 W0.1.1 C0.2.0 C0.2.1 B0 W0.2.0 W0.2.1 M0.0 M0.1 D0.0 D0.1 H0.0 H0.1
+C1.0.0 C1.0.1 L2.0 C1.1.0 C1.1.1 B1 W1.0.0 W1.0.1 C1.2.0 C1.2.1 L2.1 W1.1.0 W1.1.1 K0.0 K0.1 L2.2 W1.2.0 W1.2.1 M1.0 M1.1 D1.0 D1.1 H1.0 H1.1
+C2.0.0 C2.0.1 L3.0 X0 Y0 K1.0 K1.1 L3.1 W2.0.0 W2.0.1 C2.1.0 C2.1.1 L3.2.1 X1 Y1 C2.2.0 C2.2.1 B2 Z0.2 W2.1.0 W2.1.1 C3.0.0 C3.0.1 B3.1 W2.2.0 W2.2.1 M2.0 M2.1 D2.0 D2.1 H2.0 H2.1
+C3.1.0 C3.1.1 W3.0.0 W3.0.1 C3.2.0 W3.1.0 W3.1.1 C3.2.1 W3.2.0 M3.0 K2.0 W3.2.1 M3.1 D3.0 K2.1 H3.0 X2 Y2 K3.0 D3.1 K3.1.0 K3.1.1 H3.1 X3.0 X3.1.0 X3.1.1 Z2.3 Y3 Z3.4""".split()
+        PLAN = {"C0.0.1":0,"C1.2.1":0,"C2.2.1":0,"C3.1.1":0,"C3.2.0":44,"C3.2.1":44,"K0.1":"v","K1.1":"v","K2.1":"v","C1.1.1":0,"C2.1.1":0,"C3.0.1":0,"C0.1.1":0}
+        g_codes = [keep.tile([P, S], U32, name=f"g_codes{c}", align_bytes=64) for c in range(NP)]
+        g_scales = [keep.tile([P, S], U8, name=f"g_scales{c}", align_bytes=64) for c in range(NP)]
+        dxs = keep.tile([P, 3 * C], F32, name="dxs")
+        dxs3 = keep.tile([P, C], F32, name="dxs3")
         nc.sync.dma_start(gate_t[:], gate[0:P, :])
-        for c in range(NP):
-            dy.append(load_dy(c))
-            w2_raw[0, c] = load_w2(0, c)
-        s_t = load_saved(a1)
-        t_t = load_saved(a3)
-        w2_raw[1, 0] = load_w2(1, 0)
+        dy = {}
+        raw = {}
+        g4s = {}
+        gbs = {}
+        saved = {}
+        snegs = {}
+        sts = {}
+        wcodes = {}
+        wscales = {}
+        dhs = {}
+        das = {}
+        dac = {}
+        das_scales = {}
+        st13 = {}
+        c13 = {}
+        s13 = {}
 
-        raw13 = {}
-
-        def load_w13(e0, fine):
-            raw = ring.tile([P, 2, 2 * HP, 4, K], F32, tag="raw")
-            nc.sync.dma_start(raw[:, 0], w1[e0 : e0 + 2].rearrange("e (h p j) k -> p (e h) j k", h=HP, j=4))
-            if fine:
-                nc.sync.dma_start(raw[:, 1, 0:HP], w3[e0].rearrange("(h p j) k -> p h j k", h=HP, j=4))
-                for h in range(HP):
-                    nc.sync.dma_start(
-                        raw[:, 1, HP + h], w3[e0 + 1, 512 * h : 512 * h + 512, :].rearrange("(p j) k -> p j k", j=4)
+        def step(tok):
+            k = tok[0]
+            a = [int(x) for x in tok[1:].split(".")]
+            if k == "l":
+                c = a[0]
+                view = dyT[512 * c : 512 * c + 512, :].rearrange("(p j) t -> p j t", j=4)
+                for j in range(4):
+                    row = dy_pool.tile([P, T], F32, tag="dy", align_bytes=64)
+                    nc.sync.dma_start(row[:], view[:, j, :])
+                    dy[c, j] = row
+            elif k == "L":
+                e, c = a[0], a[1]
+                t = ring.tile([P, 4, H], F32, tag="raw")
+                view = w2[e, 512 * c : 512 * c + 512, :].rearrange("(p j) i -> p j i", j=4)
+                if len(a) > 2:
+                    for h in range(HP):
+                        nc.sync.dma_start(t[:, :, 512 * h : 512 * h + 512], view[:, :, 512 * h : 512 * h + 512])
+                else:
+                    nc.sync.dma_start(t[:], view)
+                raw[e, c] = t
+            elif k == "A":
+                m, h = a
+                if (m, 0) not in saved:
+                    t = ring.tile([P, HP, 4, S], F32, tag="raw")
+                    for hh in range(HP):
+                        saved[m, hh] = t[:, hh]
+                src = (a1, a3)[m]
+                nc.sync.dma_start(saved[m, h], src[512 * h : 512 * h + 512, :].rearrange("(p j) s -> p j s", j=4))
+            elif k == "B":
+                e = a[0]
+                t = ring.tile([P, 2, HP, 4, K], F32, tag="raw")
+                for m, w in ((0, w1), (1, w3)):
+                    if len(a) > 1 and m == 1:
+                        for h in range(HP):
+                            nc.sync.dma_start(t[:, m, h], w[e, 512 * h : 512 * h + 512, :].rearrange("(p j) k -> p j k", j=4))
+                    else:
+                        nc.sync.dma_start(t[:, m], w[e].rearrange("(h p j) k -> p h j k", h=HP, j=4))
+                raw["w", e] = t
+            elif k == "G":
+                c, half = a
+                cols = slice(256 * half, 256 * half + 256)
+                g4 = work.tile([P, 4, 256], F32)
+                for j in range(4):
+                    nc.vector.tensor_tensor(
+                        g4[:, j, :], dy[c, j][:].indirect(offsets[:, 16 * half : 16 * half + 16]), gate_t[:, cols], MULT
                     )
-            else:
-                nc.sync.dma_start(raw[:, 1], w3[e0 : e0 + 2].rearrange("e (h p j) k -> p (e h) j k", h=HP, j=4))
-            raw13[e0] = raw
-
-        def issue(load):
-            if load is None:
-                return
-            if load[0] == "w2":
-                w2_raw[load[1], load[2]] = load_w2(load[1], load[2], load[1:] == (3, 2))
-            else:
-                load_w13(load[1], load[1] == 2)
-
-        ALLS = [("s", 0, 128)]
-        ALLV = [("v", 0, 128)]
-        plan = {
-            0: [ALLS, ALLV, ALLS, ALLS, ALLS, ALLS],
-            1: [ALLS, ALLS, ALLS, ALLS, ALLS, ALLV],
-            2: [ALLS, ALLS, ALLS, ALLS, ALLS, ALLV],
-            3: [ALLS, ALLS, ALLS, ALLV, ALLS, [("s", 0, 44), ("v", 44, 128)]],
-        }
-        w2_codes = {e: ([], []) for e in range(E)}
-
-        def copies(e, c):
-            return [copy_w2(w2_raw[e, c], h, plan[e][2 * c + h]) for h in range(HP)]
-
-        def new_codes(e):
-            codes = codes_pool.tile([P, H], U32, align_bytes=64)
-            scales = codes_pool.tile([P, H], U8, align_bytes=64)
-            w2_codes[e][0].append(codes)
-            w2_codes[e][1].append(scales)
-
-        def quants(e, c, sts):
-            new_codes(e)
-            for h in range(HP):
-                quantize_w2(sts[h], w2_codes[e][0][c], w2_codes[e][1][c], h)
-
-        def copy_weights13(e, raw, el):
-            st = stage.tile([P, 2, HP, K, 4], BF16, tag="stage", align_bytes=64)
-            for m in range(2):
-                for h in range(HP):
-                    copy_w13(raw, st, el, m, h, "v" if m == 1 else "s")
-            return st
-
-        def quant_weights13(e, st, fine):
-            wc, ws = codes_w13(e)
-            if fine:
+                g4s[c, half] = g4
+            elif k == "R":
+                c, half = a
+                gb = stage.tile([P, 256, 4], BF16, tag="stage", align_bytes=64)
+                eng = nc.vector.tensor_copy if PLAN.get(tok, "v") == "v" else nc.scalar.copy
+                eng(gb[:].rearrange("p (c i) j -> p c j i", i=4), g4s[c, half][:].rearrange("p j (c i) -> p c j i", i=4))
+                gbs[c, half] = gb
+            elif k == "Q":
+                c, half = a
+                cols = slice(256 * half, 256 * half + 256)
                 nc.vector.quantize_mx(
-                    out=wc[:, 0].rearrange("p h k -> p (h k)").bitcast(FP8X4),
-                    scales=ws[:, 0].rearrange("p h k -> p (h k)"),
-                    in_=st[:, 0].rearrange("p h k j -> p (h k j)"),
+                    out=g_codes[c][:, cols].bitcast(FP8X4), scales=g_scales[c][:, cols], in_=gbs[c, half][:].rearrange("p s j -> p (s j)")
                 )
-                for h in range(HP):
+            elif k == "C":
+                e, c, h = a
+                st = stage.tile([P, 2048], BF16, tag="stage", align_bytes=64)
+                dst = st[:].rearrange("p (t m j) -> p m j t", t=4, j=4)
+                src = raw[e, c][:, :, 512 * h : 512 * h + 512].rearrange("p j (m t) -> p m j t", t=4)
+                cut = PLAN.get(tok, 128)
+                if cut > 0:
+                    nc.scalar.copy(dst[:, 0:cut], src[:, 0:cut])
+                if cut < 128:
+                    nc.vector.tensor_copy(dst[:, cut:128], src[:, cut:128])
+                sts[e, c, h] = st
+            elif k == "W":
+                e, c, h = a
+                if (e, c) not in wcodes:
+                    codes = codes_pool.tile([P, H], U32, align_bytes=64)
+                    scales = codes_pool.tile([P, H], U8, align_bytes=64)
+                    wcodes[e, c] = codes
+                    wscales[e, c] = scales
+                cols = slice(512 * h, 512 * h + 512)
+                nc.vector.quantize_mx(out=wcodes[e, c][:, cols].bitcast(FP8X4), scales=wscales[e, c][:, cols], in_=sts[e, c, h][:])
+            elif k == "S":
+                h = a[0]
+                sneg = work.tile([P, 4, S], F32, bufs=1)
+                nc.scalar.activation(sneg[:], saved[0, h], SIGMOID, scale=-1.0)
+                nc.scalar.activation(saved[0, h], saved[0, h], SIGMOID)
+                snegs[h] = sneg
+            elif k == "T":
+                h = a[0]
+                nc.vector.tensor_tensor(saved[1, h], snegs[h][:], saved[1, h], MULT)
+            elif k == "P":
+                h = a[0]
+                nc.vector.tensor_tensor(saved[1, h], saved[0, h], saved[1, h], MULT)
+            elif k == "M":
+                e, h = a
+                dh = psum.tile([P, 4, C], F32)
+                slots = slice(C * e, C * e + C)
+                for t in range(4):
+                    cols = slice(512 * h + 128 * t, 512 * h + 128 * t + 128)
+                    for c in range(NP):
+                        nc.tensor.matmul_mx(
+                            out=dh[:, t, :],
+                            lhsT=wcodes[e, c][:, cols].bitcast(FP8X4),
+                            lhsT_scale=wscales[e, c][:, cols],
+                            rhs=g_codes[c][:, slots].bitcast(FP8X4),
+                            rhs_scale=g_scales[c][:, slots],
+                            start=(c == 0),
+                            stop=(c == NP - 1),
+                        )
+                dhs[e, h] = dh
+            elif k == "D":
+                e, h = a
+                slots = slice(C * e, C * e + C)
+                da = work.tile([P, 2, C, 4], BF16, bufs=3, align_bytes=64)
+                for m, n in ((1, 0), (0, 1)):
+                    nc.vector.tensor_tensor(
+                        da[:, m].rearrange("p (c i) t -> p c t i", i=4),
+                        dhs[e, h][:].rearrange("p t (c i) -> p c t i", i=4),
+                        saved[n, h][:, :, slots].rearrange("p t (c i) -> p c t i", i=4),
+                        MULT,
+                    )
+                das[e, h] = da
+            elif k == "H":
+                e, h = a
+                dc = keep.tile([P, 2 * C], U32, name=f"da_codes{e}_{h}", align_bytes=64)
+                ds = keep.tile([P, 2 * C], U8, name=f"da_scales{e}_{h}", align_bytes=64)
+                nc.vector.quantize_mx(out=dc[:].bitcast(FP8X4), scales=ds[:], in_=das[e, h][:].rearrange("p m s t -> p (m s t)"))
+                dac[e, h] = dc
+                das_scales[e, h] = ds
+            elif k == "K":
+                e = a[0]
+                if e not in st13:
+                    st = stage.tile([P, 2, HP, K, 4], BF16, tag="stage", align_bytes=64)
+                    st13[e] = st
+                todo = [(a[1], h) for h in range(HP)] if len(a) == 2 else [(a[1], a[2])]
+                for m, h in todo:
+                    eng = nc.scalar.copy if PLAN.get(tok, "s") == "s" else nc.vector.tensor_copy
+                    eng(
+                        st13[e][:, m, h].rearrange("p (c i) j -> p c j i", i=4),
+                        raw["w", e][:, m, h].rearrange("p j (c i) -> p c j i", i=4),
+                    )
+            elif k == "X":
+                e = a[0]
+                if e not in c13:
+                    wc = dy_pool.tile([P, 2, HP, K], U32, tag="dy", align_bytes=64)
+                    ws = keep.tile([P, 2, HP, K], U8, name=f"w13_scales{e}", align_bytes=64)
+                    c13[e] = wc
+                    s13[e] = ws
+                wc, ws, st = c13[e], s13[e], st13[e]
+                if len(a) == 1:
                     nc.vector.quantize_mx(
-                        out=wc[:, 1, h].bitcast(FP8X4), scales=ws[:, 1, h], in_=st[:, 1, h].rearrange("p k j -> p (k j)")
+                        out=wc[:].rearrange("p m h k -> p (m h k)").bitcast(FP8X4),
+                        scales=ws[:].rearrange("p m h k -> p (m h k)"),
+                        in_=st[:].rearrange("p m h k j -> p (m h k j)"),
                     )
-            else:
-                nc.vector.quantize_mx(
-                    out=wc[:].rearrange("p m h k -> p (m h k)").bitcast(FP8X4),
-                    scales=ws[:].rearrange("p m h k -> p (m h k)"),
-                    in_=st[:].rearrange("p m h k j -> p (m h k j)"),
-                )
-            return wc, ws
+                elif len(a) == 2:
+                    m = a[1]
+                    nc.vector.quantize_mx(
+                        out=wc[:, m].rearrange("p h k -> p (h k)").bitcast(FP8X4),
+                        scales=ws[:, m].rearrange("p h k -> p (h k)"),
+                        in_=st[:, m].rearrange("p h k j -> p (h k j)"),
+                    )
+                else:
+                    m, h = a[1], a[2]
+                    nc.vector.quantize_mx(out=wc[:, m, h].bitcast(FP8X4), scales=ws[:, m, h], in_=st[:, m, h].rearrange("p k j -> p (k j)"))
+            elif k == "Y":
+                e = a[0]
+                dx = psum_dx.tile([P, C], F32)
+                order = [(m, h) for m in range(2) for h in range(HP)]
+                for n, (m, h) in enumerate(order):
+                    nc.tensor.matmul_mx(
+                        out=dx[:],
+                        lhsT=c13[e][:, m, h, :].bitcast(FP8X4),
+                        lhsT_scale=s13[e][:, m, h, :],
+                        rhs=dac[e, h][:, C * m : C * m + C].bitcast(FP8X4),
+                        rhs_scale=das_scales[e, h][:, C * m : C * m + C],
+                        start=(n == 0),
+                        stop=(n == len(order) - 1),
+                    )
+                nc.scalar.copy(dxs3[:] if e == 3 else dxs[:, C * e : C * e + C], dx[:])
+            elif k == "Z":
+                e0, e1 = a
+                src = dxs3[:] if e0 == 3 else dxs[:, C * e0 : C * e1]
+                nc.vector.tensor_copy(out_t[:].indirect(offsets[:, 8 * e0 : 8 * e1]), src)
 
-        loads0 = [("w2", 1, 1), ("w2", 1, 2), ("w13", 0)]
-        gathers = [(c, half) for half in range(2) for c in range(NP)]
-        prev_g = None
-        prev_w = None
-        for n, (c, half) in enumerate(gathers):
-            g4 = gather(c, half)
-            if n < NP:
-                sts = copies(0, n)
-                issue(loads0[n])
-            gb = round_g(g4)
-            if prev_g is not None:
-                quantize_g(prev_g[0], prev_g[1], prev_g[2])
-            if prev_w is not None:
-                quants(0, prev_w[0], prev_w[1])
-            prev_g = (c, half, gb)
-            prev_w = (n, sts) if n < NP else None
-        for h in range(HP):
-            for j in range(4):
-                sneg = work.tile([P, S], F32)
-                nc.scalar.activation(sneg[:], s_t[:, h, j], SIGMOID, scale=-1.0)
-                nc.vector.tensor_tensor(t_t[:, h, j], sneg[:], t_t[:, h, j], MULT)
-                if h == 0 and j == 0:
-                    quantize_g(prev_g[0], prev_g[1], prev_g[2])
-            nc.scalar.activation(s_t[:, h], s_t[:, h], SIGMOID)
-        for h in range(HP):
-            nc.vector.tensor_tensor(t_t[:, h], s_t[:, h], t_t[:, h], MULT)
-
-        loads1 = [("w2", 2, 0), ("w2", 2, 1), ("w2", 2, 2)]
-        for c in range(NP):
-            now = copies(1, c)
-            issue(loads1[c])
-            if c == 0:
-                hidden(0)
-            else:
-                quants(1, c - 1, sts)
-            sts = now
-        st13 = [copy_weights13(0, raw13[0], 0), None]
-        quants(1, 2, sts)
-        st13[1] = copy_weights13(1, raw13[0], 1)
-        issue(("w2", 3, 0))
-        w13 = [quant_weights13(0, st13[0], False), None]
-        loads2 = [("w2", 3, 1), ("w2", 3, 2), ("w13", 2)]
-        dxs01 = keep.tile([P, 2 * C], F32, name="dxs01")
-        for c in range(NP):
-            now = copies(2, c)
-            issue(loads2[c])
-            if c == 0:
-                hidden(1)
-                w13[1] = quant_weights13(1, st13[1], False)
-                down(0, w13[0][0], w13[0][1], dxs01, 0)
-                down(1, w13[1][0], w13[1][1], dxs01, C)
-            else:
-                quants(2, c - 1, sts)
-            if c == 1:
-                scatter(dxs01, 0, 2)
-            sts = now
-        for c in range(NP):
-            now = copies(3, c)
-            if c == 0:
-                quants(2, 2, sts)
-            else:
-                quants(3, c - 1, sts)
-            if c == 1:
-                hidden(2)
-            sts = now
-        quants(3, 2, sts)
-        st2 = copy_weights13(2, raw13[2], 0)
-        hidden(3)
-        wc2, ws2 = quant_weights13(2, st2, False)
-        dxs2 = work.tile([P, C], F32, tag="dxs")
-        down(2, wc2, ws2, dxs2, 0)
-        st3 = copy_weights13(3, raw13[2], 1)
-        scatter(dxs2, 2, 1)
-        wc3, ws3 = quant_weights13(3, st3, True)
-        dxs3 = work.tile([P, C], F32, tag="dxs")
-        down(3, wc3, ws3, dxs3, 0)
-        scatter(dxs3, 3, 1)
+        for tok in ORDER:
+            step(tok)
         nc.sync.dma_start(out, out_t[:])

from contextlib import ExitStack

import concourse.mybir as mybir

P = 128
E, C, K, T, H, N = 4, 128, 128, 640, 1024, 1536
S = E * C
NP = N // 512
HP = H // 512

FLOPS = 2 * S * (N * H + 2 * H * K)
BYTES = 4 * (N * T + 2 * H * S + E * N * H + 2 * E * H * K + S + K * T) + 2 * P * S // 16

F32 = mybir.dt.float32
BF16 = mybir.dt.bfloat16
U32 = mybir.dt.uint32
U16 = mybir.dt.uint16
U8 = mybir.dt.uint8
FP8X4 = mybir.dt.float8_e4m3fn_x4
MULT = mybir.AluOpType.mult
SIGMOID = mybir.ActivationFunctionType.Sigmoid


def tile_moe_bdx_glu_sigmoid_kernel(tc, dyT, a1, a3, w2, w1, w3, gate, offs, out):
    nc = tc.nc
    with ExitStack() as ctx:
        keep = ctx.enter_context(tc.tile_pool(name="keep", bufs=1))
        ring = ctx.enter_context(tc.tile_pool(name="ring", bufs=6))
        stage = ctx.enter_context(tc.tile_pool(name="stage", bufs=6))
        dy_pool = ctx.enter_context(tc.tile_pool(name="dy", bufs=12))
        codes_pool = ctx.enter_context(tc.tile_pool(name="codes", bufs=6))
        work = ctx.enter_context(tc.tile_pool(name="work", bufs=2))
        psum = ctx.enter_context(tc.psum_pool(name="psum", bufs=6))
        psum_dx = ctx.enter_context(tc.psum_pool(name="psum_dx", bufs=2))

        offsets = keep.tile([P, S // 16], U16, name="offsets")
        nc.sync.dma_start(offsets[:], offs)
        gate_t = keep.tile([P, S], F32, name="gate_t")
        out_t = keep.tile([P, T], F32, name="out_t")
        nc.gpsimd.memset(out_t[:], 0.0)
        warm = keep.tile([P, 1], F32, name="warm")
        nc.gpsimd.memset(warm[:], 0.0)
        nc.scalar.activation(warm[:], warm[:], SIGMOID)

        ORDER = """l0 L0.0 l1 A0.0 A1.0 l2 L0.1 A0.1 A1.1 L0.2 L1.0
G0.0 G0.1 R0.0 R0.1 C0.0.0 C0.0.1 L1.1 Q0.0 Q0.1 S0 G1.0 G1.1 T0 R1.0 R1.1 P0 W0.0.0 W0.0.1 Q1.0 Q1.1 G2.0 G2.1 C0.1.0 C0.1.1 L1.2 R2.0 R2.1 S1 T1 Q2.0 Q2.1 P1 W0.1.0 W0.1.1 C0.2.0 C0.2.1 B0 W0.2.0 W0.2.1 M0.0 M0.1 D0.0 D0.1 H0.0 H0.1
C1.0.0 C1.0.1 L2.0 C1.1.0 C1.1.1 B1 W1.0.0 W1.0.1 C1.2.0 C1.2.1 L2.1 W1.1.0 W1.1.1 K0.0 K0.1 L2.2 W1.2.0 W1.2.1 M1.0 M1.1 D1.0 D1.1 H1.0 H1.1
C2.0.0 C2.0.1 L3.0 X0 Y0 K1.0 K1.1 L3.1 W2.0.0 W2.0.1 C2.1.0 C2.1.1 L3.2.1 X1 Y1 C2.2.0 C2.2.1 B2 Z0.2 W2.1.0 W2.1.1 C3.0.0 C3.0.1 B3.1 W2.2.0 W2.2.1 M2.0 M2.1 D2.0 D2.1 H2.0 H2.1
C3.1.0 C3.1.1 W3.0.0 W3.0.1 C3.2.0 W3.1.0 W3.1.1 C3.2.1 W3.2.0 M3.0 K2.0 W3.2.1 M3.1 D3.0 K2.1 H3.0 X2 Y2 K3.0 D3.1 K3.1.0 K3.1.1 H3.1 X3.0 X3.1.0 X3.1.1 Z2.3 Y3 Z3.4""".split()
        PLAN = {"C0.0.1":0,"C1.2.1":0,"C2.2.1":0,"C3.1.1":0,"C3.2.0":44,"C3.2.1":44,"K0.1":"v","K1.1":"v","K2.1":"v","C1.1.1":0,"C2.1.1":0,"C3.0.1":0,"C0.1.1":0}
        g_codes = [keep.tile([P, S], U32, name=f"g_codes{c}", align_bytes=64) for c in range(NP)]
        g_scales = [keep.tile([P, S], U8, name=f"g_scales{c}", align_bytes=64) for c in range(NP)]
        dxs = keep.tile([P, 3 * C], F32, name="dxs")
        dxs3 = keep.tile([P, C], F32, name="dxs3")
        nc.sync.dma_start(gate_t[:], gate[0:P, :])
        dy = {}
        raw = {}
        g4s = {}
        gbs = {}
        saved = {}
        snegs = {}
        sts = {}
        wcodes = {}
        wscales = {}
        dhs = {}
        das = {}
        dac = {}
        das_scales = {}
        st13 = {}
        c13 = {}
        s13 = {}

        def step(tok):
            k = tok[0]
            a = [int(x) for x in tok[1:].split(".")]
            if k == "l":
                c = a[0]
                view = dyT[512 * c : 512 * c + 512, :].rearrange("(p j) t -> p j t", j=4)
                for j in range(4):
                    row = dy_pool.tile([P, T], F32, tag="dy", align_bytes=64)
                    nc.sync.dma_start(row[:], view[:, j, :])
                    dy[c, j] = row
            elif k == "L":
                e, c = a[0], a[1]
                t = ring.tile([P, 4, H], F32, tag="raw")
                view = w2[e, 512 * c : 512 * c + 512, :].rearrange("(p j) i -> p j i", j=4)
                if len(a) > 2:
                    for h in range(HP):
                        nc.sync.dma_start(t[:, :, 512 * h : 512 * h + 512], view[:, :, 512 * h : 512 * h + 512])
                else:
                    nc.sync.dma_start(t[:], view)
                raw[e, c] = t
            elif k == "A":
                m, h = a
                if (m, 0) not in saved:
                    t = ring.tile([P, HP, 4, S], F32, tag="raw")
                    for hh in range(HP):
                        saved[m, hh] = t[:, hh]
                src = (a1, a3)[m]
                nc.sync.dma_start(saved[m, h], src[512 * h : 512 * h + 512, :].rearrange("(p j) s -> p j s", j=4))
            elif k == "B":
                e = a[0]
                t = ring.tile([P, 2, HP, 4, K], F32, tag="raw")
                for m, w in ((0, w1), (1, w3)):
                    if len(a) > 1 and m == 1:
                        for h in range(HP):
                            nc.sync.dma_start(t[:, m, h], w[e, 512 * h : 512 * h + 512, :].rearrange("(p j) k -> p j k", j=4))
                    else:
                        nc.sync.dma_start(t[:, m], w[e].rearrange("(h p j) k -> p h j k", h=HP, j=4))
                raw["w", e] = t
            elif k == "G":
                c, half = a
                cols = slice(256 * half, 256 * half + 256)
                g4 = work.tile([P, 4, 256], F32)
                for j in range(4):
                    nc.vector.tensor_tensor(
                        g4[:, j, :], dy[c, j][:].indirect(offsets[:, 16 * half : 16 * half + 16]), gate_t[:, cols], MULT
                    )
                g4s[c, half] = g4
            elif k == "R":
                c, half = a
                gb = stage.tile([P, 256, 4], BF16, tag="stage", align_bytes=64)
                eng = nc.vector.tensor_copy if PLAN.get(tok, "v") == "v" else nc.scalar.copy
                eng(gb[:].rearrange("p (c i) j -> p c j i", i=4), g4s[c, half][:].rearrange("p j (c i) -> p c j i", i=4))
                gbs[c, half] = gb
            elif k == "Q":
                c, half = a
                cols = slice(256 * half, 256 * half + 256)
                nc.vector.quantize_mx(
                    out=g_codes[c][:, cols].bitcast(FP8X4), scales=g_scales[c][:, cols], in_=gbs[c, half][:].rearrange("p s j -> p (s j)")
                )
            elif k == "C":
                e, c, h = a
                st = stage.tile([P, 2048], BF16, tag="stage", align_bytes=64)
                dst = st[:].rearrange("p (t m j) -> p m j t", t=4, j=4)
                src = raw[e, c][:, :, 512 * h : 512 * h + 512].rearrange("p j (m t) -> p m j t", t=4)
                cut = PLAN.get(tok, 128)
                if cut > 0:
                    nc.scalar.copy(dst[:, 0:cut], src[:, 0:cut])
                if cut < 128:
                    nc.vector.tensor_copy(dst[:, cut:128], src[:, cut:128])
                sts[e, c, h] = st
            elif k == "W":
                e, c, h = a
                if (e, c) not in wcodes:
                    codes = codes_pool.tile([P, H], U32, align_bytes=64)
                    scales = codes_pool.tile([P, H], U8, align_bytes=64)
                    wcodes[e, c] = codes
                    wscales[e, c] = scales
                cols = slice(512 * h, 512 * h + 512)
                nc.vector.quantize_mx(out=wcodes[e, c][:, cols].bitcast(FP8X4), scales=wscales[e, c][:, cols], in_=sts[e, c, h][:])
            elif k == "S":
                h = a[0]
                sneg = work.tile([P, 4, S], F32, bufs=1)
                nc.scalar.activation(sneg[:], saved[0, h], SIGMOID, scale=-1.0)
                nc.scalar.activation(saved[0, h], saved[0, h], SIGMOID)
                snegs[h] = sneg
            elif k == "T":
                h = a[0]
                nc.vector.tensor_tensor(saved[1, h], snegs[h][:], saved[1, h], MULT)
            elif k == "P":
                h = a[0]
                nc.vector.tensor_tensor(saved[1, h], saved[0, h], saved[1, h], MULT)
            elif k == "M":
                e, h = a
                dh = psum.tile([P, 4, C], F32)
                slots = slice(C * e, C * e + C)
                for t in range(4):
                    cols = slice(512 * h + 128 * t, 512 * h + 128 * t + 128)
                    for c in range(NP):
                        nc.tensor.matmul_mx(
                            out=dh[:, t, :],
                            lhsT=wcodes[e, c][:, cols].bitcast(FP8X4),
                            lhsT_scale=wscales[e, c][:, cols],
                            rhs=g_codes[c][:, slots].bitcast(FP8X4),
                            rhs_scale=g_scales[c][:, slots],
                            start=(c == 0),
                            stop=(c == NP - 1),
                        )
                dhs[e, h] = dh
            elif k == "D":
                e, h = a
                slots = slice(C * e, C * e + C)
                da = work.tile([P, 2, C, 4], BF16, bufs=3, align_bytes=64)
                for m, n in ((1, 0), (0, 1)):
                    nc.vector.tensor_tensor(
                        da[:, m].rearrange("p (c i) t -> p c t i", i=4),
                        dhs[e, h][:].rearrange("p t (c i) -> p c t i", i=4),
                        saved[n, h][:, :, slots].rearrange("p t (c i) -> p c t i", i=4),
                        MULT,
                    )
                das[e, h] = da
            elif k == "H":
                e, h = a
                dc = keep.tile([P, 2 * C], U32, name=f"da_codes{e}_{h}", align_bytes=64)
                ds = keep.tile([P, 2 * C], U8, name=f"da_scales{e}_{h}", align_bytes=64)
                nc.vector.quantize_mx(out=dc[:].bitcast(FP8X4), scales=ds[:], in_=das[e, h][:].rearrange("p m s t -> p (m s t)"))
                dac[e, h] = dc
                das_scales[e, h] = ds
            elif k == "K":
                e = a[0]
                if e not in st13:
                    st = stage.tile([P, 2, HP, K, 4], BF16, tag="stage", align_bytes=64)
                    st13[e] = st
                todo = [(a[1], h) for h in range(HP)] if len(a) == 2 else [(a[1], a[2])]
                for m, h in todo:
                    eng = nc.scalar.copy if PLAN.get(tok, "s") == "s" else nc.vector.tensor_copy
                    eng(
                        st13[e][:, m, h].rearrange("p (c i) j -> p c j i", i=4),
                        raw["w", e][:, m, h].rearrange("p j (c i) -> p c j i", i=4),
                    )
            elif k == "X":
                e = a[0]
                if e not in c13:
                    wc = dy_pool.tile([P, 2, HP, K], U32, tag="dy", align_bytes=64)
                    ws = keep.tile([P, 2, HP, K], U8, name=f"w13_scales{e}", align_bytes=64)
                    c13[e] = wc
                    s13[e] = ws
                wc, ws, st = c13[e], s13[e], st13[e]
                if len(a) == 1:
                    nc.vector.quantize_mx(
                        out=wc[:].rearrange("p m h k -> p (m h k)").bitcast(FP8X4),
                        scales=ws[:].rearrange("p m h k -> p (m h k)"),
                        in_=st[:].rearrange("p m h k j -> p (m h k j)"),
                    )
                elif len(a) == 2:
                    m = a[1]
                    nc.vector.quantize_mx(
                        out=wc[:, m].rearrange("p h k -> p (h k)").bitcast(FP8X4),
                        scales=ws[:, m].rearrange("p h k -> p (h k)"),
                        in_=st[:, m].rearrange("p h k j -> p (h k j)"),
                    )
                else:
                    m, h = a[1], a[2]
                    nc.vector.quantize_mx(out=wc[:, m, h].bitcast(FP8X4), scales=ws[:, m, h], in_=st[:, m, h].rearrange("p k j -> p (k j)"))
            elif k == "Y":
                e = a[0]
                dx = psum_dx.tile([P, C], F32)
                order = [(m, h) for m in range(2) for h in range(HP)]
                for n, (m, h) in enumerate(order):
                    nc.tensor.matmul_mx(
                        out=dx[:],
                        lhsT=c13[e][:, m, h, :].bitcast(FP8X4),
                        lhsT_scale=s13[e][:, m, h, :],
                        rhs=dac[e, h][:, C * m : C * m + C].bitcast(FP8X4),
                        rhs_scale=das_scales[e, h][:, C * m : C * m + C],
                        start=(n == 0),
                        stop=(n == len(order) - 1),
                    )
                nc.scalar.copy(dxs3[:] if e == 3 else dxs[:, C * e : C * e + C], dx[:])
            elif k == "Z":
                e0, e1 = a
                src = dxs3[:] if e0 == 3 else dxs[:, C * e0 : C * e1]
                nc.vector.tensor_copy(out_t[:].indirect(offsets[:, 8 * e0 : 8 * e1]), src)

        for tok in ORDER:
            step(tok)
        nc.sync.dma_start(out, out_t[:])
